import numpy as np
import ml_dtypes


def mxq(x, axis, fmt="e4m3"):
    dtype, down = {"e4m3": (ml_dtypes.float8_e4m3fn, 7), "e5m2": (ml_dtypes.float8_e5m2, 14)}[fmt]
    v = np.moveaxis(np.asarray(x, np.float32).astype(ml_dtypes.bfloat16).astype(np.float64), axis, -1)
    blocks = v.reshape(v.shape[:-1] + (-1, 32))
    amax = np.abs(blocks).max(-1, keepdims=True)
    byte = np.maximum(np.where(amax > 0, np.frexp(amax)[1] - 1 + 127, 0) - down, 1)
    scale = np.exp2(byte - 127.0)
    codes = (blocks / scale).astype(np.float32).astype(dtype).astype(np.float64)
    return np.moveaxis((codes * scale).reshape(v.shape), -1, axis)


WIDE = False


def mx_kscale(k):
    if not WIDE:
        return np.ones(k)
    levels = np.array([18, -18])
    if k % 512:
        return np.exp2(np.random.permutation(np.resize(levels, k // 32))).repeat(32)
    a = np.empty((k // 512, 16))
    for p in range(k // 512):
        a[p, :8] = np.random.permutation(np.resize(levels, 8))
        for g in range(8):
            far = levels[np.abs(levels - a[p, g]) >= 10]
            a[p, g + 8] = far[np.random.randint(len(far))]
    return np.exp2(a.ravel()).repeat(32)


def f64(x):
    return np.asarray(x).astype(np.float64)


def striped(idx):
    return np.tile(np.asarray(idx).reshape(-1, 16).T, (8, 1)).astype(np.uint16)


def unstriped(offs):
    return offs[:16].T.reshape(-1).astype(np.int64)


B, N, T, D, R = 2, 512, 2048, 512, 512


def setup_inputs():
    n = np.random.standard_normal
    idx = np.random.permutation(T)[:B * N]
    s = mx_kscale(D)[:, None]
    z = mx_kscale(R)[:, None]
    x = n((B, D, R))
    return {
        "xT": (x * s).astype(np.float32),
        "wT": (n((D, T)) * (0.50 / np.sqrt(D)) / s).astype(np.float32),
        "vT": (n((D, T)) / np.sqrt(D) / s).astype(np.float32),
        "wt": (np.random.uniform(0.5, 1.5, (B, R, 1)) * N / np.sqrt(R) * z).astype(np.float32),
        "xm": (x.transpose(0, 2, 1) / z).astype(np.float32),
        "offs": striped(idx),
    }


def reference(xT, wT, vT, wt, xm, offs):
    idx = unstriped(offs)
    pick = lambda x: x[:, idx].reshape(x.shape[0], B, N).transpose(1, 0, 2)
    xq = mxq(f64(xT), 1, "e4m3").transpose(0, 2, 1)
    a = xq @ mxq(pick(f64(wT)), 1, "e4m3")
    av = xq @ mxq(pick(f64(vT)), 1, "e4m3")
    e = np.exp(a - a.max(-1, keepdims=True))
    p = e / e.sum(-1, keepdims=True)
    g = f64(wt) * p * (av - (p * av).sum(-1, keepdims=True))
    dw = mxq(f64(xm), 1, "e4m3").transpose(0, 2, 1) @ mxq(g, 1, "e5m2")
    gw = np.zeros((D, T))
    gw[:, idx] = dw.transpose(1, 0, 2).reshape(D, B * N)
    return gw

@@ -1,0 +1,228 @@
+from contextlib import ExitStack
+
+import concourse.mybir as mybir
+
+B, N, T, D, R = 2, 512, 2048, 512, 512
+FLOPS = 3 * 2 * B * R * N * D
+
+F32 = mybir.dt.float32
+BF16 = mybir.dt.bfloat16
+U32 = mybir.dt.uint32
+U16 = mybir.dt.uint16
+U8 = mybir.dt.uint8
+E4M3 = mybir.dt.float8_e4m3fn_x4
+E5M2 = mybir.dt.float8_e5m2_x4
+ACT = mybir.ActivationFunctionType
+ALU = mybir.AluOpType
+AX = mybir.AxisListType
+
+P = 128
+PACK = 4
+HALF = T // 2
+LIST_COLS = N // 16
+
+
+def tile_attend_ghv_kl_kernel(tc, xT, wT, vT, wt, xm, offs, out):
+    nc = tc.nc
+    with ExitStack() as ctx:
+        keep = ctx.enter_context(tc.tile_pool(name="keep", bufs=1))
+        raw = ctx.enter_context(tc.tile_pool(name="raw", bufs=8))
+        half = ctx.enter_context(tc.tile_pool(name="half", bufs=6))
+        work = ctx.enter_context(tc.tile_pool(name="work", bufs=8))
+        psum = ctx.enter_context(tc.psum_pool(name="psum", bufs=8))
+
+        offsets = keep.tile([P, B * LIST_COLS], U16, name="offsets")
+        weights = keep.tile([P, B, PACK], F32, name="weights")
+        windows = [keep.tile([P, T], F32, name="window%d" % j) for j in range(D // P)]
+        pairs = {}
+        for name in ("w", "v"):
+            for u in range(2):
+                pairs[name, u] = keep.tile([P, 2 * T], BF16, name="pairs_%s%d" % (name, u))
+
+        def load_table(table, u, h):
+            chunk = raw.tile([P, PACK * R], F32, name="raw")
+            view = chunk[:].rearrange("p (e n) -> p e n", e=2)
+            rows = table.rearrange("(p t) n -> p t n", t=PACK)
+            nc.sync.dma_start(out=view, in_=rows[:, 2 * u : 2 * u + 2, h * HALF : (h + 1) * HALF])
+            return view
+
+        def load_x(x):
+            chunk = raw.tile([P, PACK * R], F32, name="raw")
+            view = chunk[:].rearrange("p (t c) -> p t c", t=PACK)
+            nc.sync.dma_start(out=view, in_=x.rearrange("(p t) c -> p t c", t=PACK))
+            return view
+
+        def cast_pairs(name, u, h, view, on_scalar):
+            dst = pairs[name, u][:].rearrange("p (n e) -> p n e", e=2)[:, h * HALF : (h + 1) * HALF, :]
+            src = view.rearrange("p e n -> p n e")
+            if on_scalar > 0:
+                nc.scalar.activation(out=dst[:, :on_scalar, :], in_=src[:, :on_scalar, :], func=ACT.Copy)
+            if on_scalar < HALF:
+                nc.vector.tensor_copy(out=dst[:, on_scalar:, :], in_=src[:, on_scalar:, :])
+
+        def staged():
+            return half.tile([P, PACK * N], BF16, name="staged", align_bytes=64)
+
+        def gather(name, u, b, dst):
+            words = dst[:].bitcast(U32).rearrange("p (n u) -> p n u", u=2)
+            window = pairs[name, u][:].bitcast(U32)
+            nc.vector.tensor_copy(
+                out=words[:, :, u], in_=window.indirect(offsets[:, b * LIST_COLS : (b + 1) * LIST_COLS])
+            )
+
+        def quantize(name, src, fmt):
+            codes = keep.tile([P, N], U32, name="codes_" + name, align_bytes=64)
+            scales = keep.tile([P, N], U8, name="scales_" + name, align_bytes=64)
+            nc.vector.quantize_mx(out=codes[:].bitcast(fmt), scales=scales[:], in_=src[:])
+            return codes, scales, fmt
+
+        def product(lhs, j, rhs):
+            bank = psum.tile([P, N], F32, name="bank")
+            cols = slice(j * P, (j + 1) * P)
+            nc.tensor.matmul_mx(
+                out=bank[:],
+                lhsT=lhs[0][:, cols].bitcast(lhs[2]),
+                lhsT_scale=lhs[1][:, cols],
+                rhs=rhs[0][:].bitcast(rhs[2]),
+                rhs_scale=rhs[1][:],
+                start=True,
+                stop=True,
+            )
+            return bank
+
+        def cast_xT(view):
+            dst = staged()
+            nc.scalar.activation(
+                out=dst[:].rearrange("p (s m t) -> p m s t", s=PACK, t=PACK),
+                in_=view.rearrange("p t (m s) -> p m s t", s=PACK),
+                func=ACT.Copy,
+            )
+            return dst
+
+        def cast_xm(view):
+            dst = staged()
+            nc.scalar.activation(
+                out=dst[:].rearrange("p (c i t) -> p c t i", i=4, t=PACK),
+                in_=view.rearrange("p t (c i) -> p c t i", i=4),
+                func=ACT.Copy,
+            )
+            return dst
+
+        def exponentials(b, xq, wq):
+            neg_max = keep.tile([P, PACK], F32, name="neg_max%d" % b)
+            total = keep.tile([P, PACK], F32, name="total%d" % b)
+            exps = []
+            for s in range(PACK):
+                a = product(xq, s, wq)
+                nc.vector.tensor_reduce(out=neg_max[:, s : s + 1], in_=a[:], axis=AX.X, op=ALU.max, negate=True)
+                e = work.tile([P, N], F32, name="e")
+                nc.scalar.activation(
+                    out=e[:], in_=a[:], func=ACT.Exp, bias=neg_max[:, s : s + 1], accum_out=total[:, s : s + 1]
+                )
+                exps.append(e)
+            return exps, total
+
+        def row_factors(b, total):
+            inv = keep.tile([P, PACK], F32, name="inv%d" % b)
+            nc.vector.reciprocal(out=inv[:], in_=total[:])
+            alpha = keep.tile([P, PACK], F32, name="alpha%d" % b)
+            nc.vector.tensor_tensor(out=alpha[:], in0=inv[:], in1=weights[:, b, :], op=ALU.mult)
+            return inv, alpha
+
+        def gradient(b, xq, vq, exps, inv, alpha):
+            usum = keep.tile([P, PACK], F32, name="usum%d" % b)
+            neg_beta = keep.tile([P, PACK], F32, name="neg_beta%d" % b)
+            us = []
+            for s in range(PACK):
+                av = product(xq, s, vq)
+                u = work.tile([P, N], F32, name="u", bufs=6)
+                nc.vector.scalar_tensor_tensor(
+                    out=u[:], in0=av[:], scalar=alpha[:, s : s + 1], in1=exps[s][:],
+                    op0=ALU.mult, op1=ALU.mult, accum_out=usum[:, s : s + 1],
+                )
+                us.append(u)
+                if s % 2 == 1:
+                    two = slice(s - 1, s + 1)
+                    nc.vector.scalar_tensor_tensor(
+                        out=neg_beta[:, two], in0=usum[:, two], scalar=-1.0, in1=inv[:, two],
+                        op0=ALU.mult, op1=ALU.mult,
+                    )
+            planes = staged()
+            for s in range(PACK):
+                nc.vector.scalar_tensor_tensor(
+                    out=planes[:, s * N : (s + 1) * N], in0=exps[s][:], scalar=neg_beta[:, s : s + 1],
+                    in1=us[s][:], op0=ALU.mult, op1=ALU.add,
+                )
+            g = staged()
+            nc.scalar.copy(
+                out=g[:].rearrange("p (c i s) -> p c s i", i=4, s=PACK),
+                in_=planes[:].rearrange("p (s c i) -> p c s i", i=4, s=PACK),
+            )
+            return g
+
+        def scatter(b, xmq, gq):
+            for j in range(D // P):
+                bank = product(xmq, j, gq)
+                dw = work.tile([P, N], F32, name="dw", bufs=4)
+                nc.scalar.copy(out=dw[:], in_=bank[:])
+                nc.vector.tensor_copy(
+                    out=windows[j][:].indirect(offsets[:, b * LIST_COLS : (b + 1) * LIST_COLS]), in_=dw[:]
+                )
+                if b == B - 1:
+                    nc.sync.dma_start(out=out[j * P : (j + 1) * P, :], in_=windows[j][:])
+
+        for window in windows:
+            nc.vector.memset(window[:], 0.0)
+
+        w_raw = {}
+        w_raw[0, 0] = load_table(wT, 0, 0)
+        nc.sync.dma_start(offsets[:], offs)
+        w_raw[0, 1] = load_table(wT, 0, 1)
+        w_raw[1, 0] = load_table(wT, 1, 0)
+        w_raw[1, 1] = load_table(wT, 1, 1)
+        xT0_raw = load_x(xT[0])
+        v_raw = {}
+        for u in range(2):
+            for h in range(2):
+                v_raw[u, h] = load_table(vT, u, h)
+        nc.sync.dma_start(out=weights[:], in_=wt.rearrange("b (p s) o -> p b (s o)", s=PACK))
+        xm0_raw = load_x(xm[0])
+        xT1_raw = load_x(xT[1])
+        xm1_raw = load_x(xm[1])
+
+        wg = [staged(), staged()]
+        for u in range(2):
+            cast_pairs("w", u, 0, w_raw[u, 0], HALF)
+            cast_pairs("w", u, 1, w_raw[u, 1], 384)
+            for b in range(B):
+                gather("w", u, b, wg[b])
+        xT0 = cast_xT(xT0_raw)
+        wq = [quantize("w%d" % b, wg[b], E4M3) for b in range(B)]
+        xq0 = quantize("xT0", xT0, E4M3)
+        cast_pairs("v", 0, 0, v_raw[0, 0], HALF)
+        cast_pairs("v", 0, 1, v_raw[0, 1], HALF)
+        cast_pairs("v", 1, 0, v_raw[1, 0], HALF)
+        exps0, total0 = exponentials(0, xq0, wq[0])
+        vg = [staged(), staged()]
+        for b in range(B):
+            gather("v", 0, b, vg[b])
+        cast_pairs("v", 1, 1, v_raw[1, 1], 0)
+        gather("v", 1, 0, vg[0])
+        inv0, alpha0 = row_factors(0, total0)
+        vq0 = quantize("v0", vg[0], E4M3)
+        gather("v", 1, 1, vg[1])
+        xm0 = cast_xm(xm0_raw)
+        xT1 = cast_xT(xT1_raw)
+        g0 = gradient(0, xq0, vq0, exps0, inv0, alpha0)
+        vq1 = quantize("v1", vg[1], E4M3)
+        xq1 = quantize("xT1", xT1, E4M3)
+        xmq0 = quantize("xm0", xm0, E4M3)
+        exps1, total1 = exponentials(1, xq1, wq[1])
+        gq0 = quantize("g0", g0, E5M2)
+        xm1 = cast_xm(xm1_raw)
+        inv1, alpha1 = row_factors(1, total1)
+        g1 = gradient(1, xq1, vq1, exps1, inv1, alpha1)
+        xmq1 = quantize("xm1", xm1, E4M3)
+        scatter(0, xmq0, gq0)
+        gq1 = quantize("g1", g1, E5M2)
+        scatter(1, xmq1, gq1)

@@ -26,10 +26,13 @@ def tile_attend_ghv_kl_kernel(tc, xT, wT, vT, wt, xm, offs, out):
     nc = tc.nc
     with ExitStack() as ctx:
         keep = ctx.enter_context(tc.tile_pool(name="keep", bufs=1))
-        raw = ctx.enter_context(tc.tile_pool(name="raw", bufs=8))
-        half = ctx.enter_context(tc.tile_pool(name="half", bufs=6))
-        work = ctx.enter_context(tc.tile_pool(name="work", bufs=8))
-        psum = ctx.enter_context(tc.psum_pool(name="psum", bufs=8))
+        psum = ctx.enter_context(tc.psum_pool(name="psum", bufs=1))
+        turns = {}
+
+        def next_tag(kind, depth):
+            turn = turns.get(kind, 0)
+            turns[kind] = turn + 1
+            return "%s_%d" % (kind, turn % depth)
 
         offsets = keep.tile([P, B * LIST_COLS], U16, name="offsets")
         weights = keep.tile([P, B, PACK], F32, name="weights")
@@ -37,17 +40,19 @@ def tile_attend_ghv_kl_kernel(tc, xT, wT, vT, wt, xm, offs, out):
         pairs = {}
         for name in ("w", "v"):
             for u in range(2):
-                pairs[name, u] = keep.tile([P, 2 * T], BF16, name="pairs_%s%d" % (name, u))
+                pairs[name, u] = keep.tile(
+                    [P, 2 * T], BF16, name="pairs", tag="pairs_%s%d" % (name, u), align_bytes=64
+                )
 
         def load_table(table, u, h):
-            chunk = raw.tile([P, PACK * R], F32, name="raw")
+            chunk = keep.tile([P, PACK * R], F32, name="raw", tag=next_tag("raw", 8))
             view = chunk[:].rearrange("p (e n) -> p e n", e=2)
             rows = table.rearrange("(p t) n -> p t n", t=PACK)
             nc.sync.dma_start(out=view, in_=rows[:, 2 * u : 2 * u + 2, h * HALF : (h + 1) * HALF])
             return view
 
         def load_x(x):
-            chunk = raw.tile([P, PACK * R], F32, name="raw")
+            chunk = keep.tile([P, PACK * R], F32, name="raw", tag=next_tag("raw", 8))
             view = chunk[:].rearrange("p (t c) -> p t c", t=PACK)
             nc.sync.dma_start(out=view, in_=x.rearrange("(p t) c -> p t c", t=PACK))
             return view
@@ -60,8 +65,8 @@ def tile_attend_ghv_kl_kernel(tc, xT, wT, vT, wt, xm, offs, out):
             if on_scalar < HALF:
                 nc.vector.tensor_copy(out=dst[:, on_scalar:, :], in_=src[:, on_scalar:, :])
 
-        def staged():
-            return half.tile([P, PACK * N], BF16, name="staged", align_bytes=64)
+        def staged(tag):
+            return keep.tile([P, PACK * N], BF16, name="staged", tag=tag, align_bytes=64)
 
         def gather(name, u, b, dst):
             words = dst[:].bitcast(U32).rearrange("p (n u) -> p n u", u=2)
@@ -70,6 +75,25 @@ def tile_attend_ghv_kl_kernel(tc, xT, wT, vT, wt, xm, offs, out):
                 out=words[:, :, u], in_=window.indirect(offsets[:, b * LIST_COLS : (b + 1) * LIST_COLS])
             )
 
+        def gather_plain(name, u, b, dst):
+            window = pairs[name, u][:].bitcast(U32)
+            nc.vector.tensor_copy(
+                out=dst[:].bitcast(U32)[:, u * N : (u + 1) * N],
+                in_=window.indirect(offsets[:, b * LIST_COLS : (b + 1) * LIST_COLS]),
+            )
+
+        def join_pairs(src, on_gpsimd):
+            staging = staged(next_tag("joined", 4))
+            dst = staging[:].rearrange("p (n u e) -> p n u e", u=2, e=2)
+            view = src[:].rearrange("p (u n e) -> p n u e", u=2, e=2)
+            if on_gpsimd:
+                for q in range(2):
+                    part = slice(q * N // 2, (q + 1) * N // 2)
+                    nc.gpsimd.tensor_scalar(dst[:, part], view[:, part], 1.0, 0.0, ALU.mult, ALU.add)
+            else:
+                nc.scalar.copy(out=dst, in_=view)
+            return staging
+
         def quantize(name, src, fmt):
             codes = keep.tile([P, N], U32, name="codes_" + name, align_bytes=64)
             scales = keep.tile([P, N], U8, name="scales_" + name, align_bytes=64)
@@ -77,7 +101,7 @@ def tile_attend_ghv_kl_kernel(tc, xT, wT, vT, wt, xm, offs, out):
             return codes, scales, fmt
 
         def product(lhs, j, rhs):
-            bank = psum.tile([P, N], F32, name="bank")
+            bank = psum.tile([P, N], F32, name="bank", tag=next_tag("bank%d" % j, 2))
             cols = slice(j * P, (j + 1) * P)
             nc.tensor.matmul_mx(
                 out=bank[:],
@@ -90,36 +114,34 @@ def tile_attend_ghv_kl_kernel(tc, xT, wT, vT, wt, xm, offs, out):
             )
             return bank
 
-        def cast_xT(view):
-            dst = staged()
-            nc.scalar.activation(
-                out=dst[:].rearrange("p (s m t) -> p m s t", s=PACK, t=PACK),
-                in_=view.rearrange("p t (m s) -> p m s t", s=PACK),
-                func=ACT.Copy,
-            )
-            return dst
-
-        def cast_xm(view):
-            dst = staged()
-            nc.scalar.activation(
-                out=dst[:].rearrange("p (c i t) -> p c t i", i=4, t=PACK),
-                in_=view.rearrange("p t (c i) -> p c t i", i=4),
-                func=ACT.Copy,
-            )
-            return dst
+        def cast_x(view, b, turned, aside, on_gpsimd, parts):
+            staging = staged("x%d" % b)
+            if turned:
+                dst = staging[:].rearrange("p (s m t) -> p m s t", s=PACK, t=PACK)
+                src = view.rearrange("p t (m s) -> p m s t", s=PACK)
+            else:
+                dst = staging[:].rearrange("p (c i t) -> p c t i", i=4, t=PACK)
+                src = view.rearrange("p t (c i) -> p c t i", i=4)
+            for q in range(parts if aside else 0):
+                part = slice(q * aside // parts, (q + 1) * aside // parts)
+                if on_gpsimd:
+                    nc.gpsimd.tensor_scalar(dst[:, part], src[:, part], 1.0, 0.0, ALU.mult, ALU.add)
+                else:
+                    nc.scalar.activation(out=dst[:, part], in_=src[:, part], func=ACT.Copy)
+            if aside < P:
+                nc.vector.tensor_copy(out=dst[:, aside:], in_=src[:, aside:])
+            return staging
 
         def exponentials(b, xq, wq):
             neg_max = keep.tile([P, PACK], F32, name="neg_max%d" % b)
             total = keep.tile([P, PACK], F32, name="total%d" % b)
-            exps = []
+            exps = keep.tile([P, PACK, N], F32, name="exps%d" % b, tag="exps%d" % b)
             for s in range(PACK):
                 a = product(xq, s, wq)
                 nc.vector.tensor_reduce(out=neg_max[:, s : s + 1], in_=a[:], axis=AX.X, op=ALU.max, negate=True)
-                e = work.tile([P, N], F32, name="e")
                 nc.scalar.activation(
-                    out=e[:], in_=a[:], func=ACT.Exp, bias=neg_max[:, s : s + 1], accum_out=total[:, s : s + 1]
+                    out=exps[:, s, :], in_=a[:], func=ACT.Exp, bias=neg_max[:, s : s + 1], accum_out=total[:, s : s + 1]
                 )
-                exps.append(e)
             return exps, total
 
         def row_factors(b, total):
@@ -131,98 +153,132 @@ def tile_attend_ghv_kl_kernel(tc, xT, wT, vT, wt, xm, offs, out):
 
         def gradient(b, xq, vq, exps, inv, alpha):
             usum = keep.tile([P, PACK], F32, name="usum%d" % b)
+            beta = keep.tile([P, PACK], F32, name="beta%d" % b)
+            u = keep.tile([P, PACK, N], F32, name="u%d" % b, tag="u%d" % b)
+            for s in range(PACK):
+                col = slice(s, s + 1)
+                av = product(xq, s, vq)
+                nc.vector.scalar_tensor_tensor(
+                    out=u[:, s, :], in0=av[:], scalar=alpha[:, col], in1=exps[:, s, :],
+                    op0=ALU.mult, op1=ALU.mult, accum_out=usum[:, col],
+                )
+                nc.scalar.activation(out=beta[:, col], in_=usum[:, col], func=ACT.Copy, scale=inv[:, col])
+                nc.scalar.activation(out=exps[:, s, :], in_=exps[:, s, :], func=ACT.Copy, scale=beta[:, col])
+            g = staged("pairs_w%d" % b)
+            dst = g[:].rearrange("p (c i s) -> p c s i", i=4, s=PACK)
+            in0 = u[:].rearrange("p s (c i) -> p c s i", i=4)
+            in1 = exps[:].rearrange("p s (c i) -> p c s i", i=4)
+            for q in range(4):
+                part = slice(32 * q, 32 * (q + 1))
+                nc.gpsimd.tensor_tensor(out=dst[:, part], in0=in0[:, part], in1=in1[:, part], op=ALU.subtract)
+            return g
+
+        def gradient_on_vector(b, xq, vq, exps, inv, alpha):
+            usum = keep.tile([P, PACK], F32, name="usum%d" % b)
             neg_beta = keep.tile([P, PACK], F32, name="neg_beta%d" % b)
-            us = []
+            u = keep.tile([P, PACK, N], F32, name="u%d" % b, tag="u%d" % b)
             for s in range(PACK):
                 av = product(xq, s, vq)
-                u = work.tile([P, N], F32, name="u", bufs=6)
                 nc.vector.scalar_tensor_tensor(
-                    out=u[:], in0=av[:], scalar=alpha[:, s : s + 1], in1=exps[s][:],
+                    out=u[:, s, :], in0=av[:], scalar=alpha[:, s : s + 1], in1=exps[:, s, :],
                     op0=ALU.mult, op1=ALU.mult, accum_out=usum[:, s : s + 1],
                 )
-                us.append(u)
                 if s % 2 == 1:
                     two = slice(s - 1, s + 1)
                     nc.vector.scalar_tensor_tensor(
                         out=neg_beta[:, two], in0=usum[:, two], scalar=-1.0, in1=inv[:, two],
                         op0=ALU.mult, op1=ALU.mult,
                     )
-            planes = staged()
+            planes = staged("planes")
             for s in range(PACK):
                 nc.vector.scalar_tensor_tensor(
-                    out=planes[:, s * N : (s + 1) * N], in0=exps[s][:], scalar=neg_beta[:, s : s + 1],
-                    in1=us[s][:], op0=ALU.mult, op1=ALU.add,
+                    out=planes[:, s * N : (s + 1) * N], in0=exps[:, s, :], scalar=neg_beta[:, s : s + 1],
+                    in1=u[:, s, :], op0=ALU.mult, op1=ALU.add,
                 )
-            g = staged()
+            g = staged("pairs_w%d" % b)
             nc.scalar.copy(
                 out=g[:].rearrange("p (c i s) -> p c s i", i=4, s=PACK),
                 in_=planes[:].rearrange("p (s c i) -> p c s i", i=4, s=PACK),
             )
             return g
 
-        def scatter(b, xmq, gq):
-            for j in range(D // P):
-                bank = product(xmq, j, gq)
-                dw = work.tile([P, N], F32, name="dw", bufs=4)
-                nc.scalar.copy(out=dw[:], in_=bank[:])
-                nc.vector.tensor_copy(
-                    out=windows[j][:].indirect(offsets[:, b * LIST_COLS : (b + 1) * LIST_COLS]), in_=dw[:]
-                )
-                if b == B - 1:
-                    nc.sync.dma_start(out=out[j * P : (j + 1) * P, :], in_=windows[j][:])
+        def scatter(b, j, xmq, gq, tag):
+            bank = product(xmq, j, gq)
+            if tag:
+                dw = keep.tile([P, N], F32, name="dw_late", tag=tag)
+            else:
+                dw = keep.tile([P, N], F32, name="dw", tag=next_tag("dw", 4))
+            nc.scalar.copy(out=dw[:], in_=bank[:])
+            nc.vector.tensor_copy(
+                out=windows[j][:].indirect(offsets[:, b * LIST_COLS : (b + 1) * LIST_COLS]), in_=dw[:]
+            )
+            if b == B - 1:
+                nc.sync.dma_start(out=out[j * P : (j + 1) * P, :], in_=windows[j][:])
 
         for window in windows:
             nc.vector.memset(window[:], 0.0)
 
-        w_raw = {}
-        w_raw[0, 0] = load_table(wT, 0, 0)
+        r_w00 = load_table(wT, 0, 0)
         nc.sync.dma_start(offsets[:], offs)
-        w_raw[0, 1] = load_table(wT, 0, 1)
-        w_raw[1, 0] = load_table(wT, 1, 0)
-        w_raw[1, 1] = load_table(wT, 1, 1)
-        xT0_raw = load_x(xT[0])
-        v_raw = {}
-        for u in range(2):
-            for h in range(2):
-                v_raw[u, h] = load_table(vT, u, h)
+        r_w01 = load_table(wT, 0, 1)
+        r_w10 = load_table(wT, 1, 0)
+        r_w11 = load_table(wT, 1, 1)
+        r_xT0 = load_x(xT[0])
+        r_xT1 = load_x(xT[1])
+        r_v10 = load_table(vT, 1, 0)
+        r_v11 = load_table(vT, 1, 1)
+        r_v01 = load_table(vT, 0, 1)
         nc.sync.dma_start(out=weights[:], in_=wt.rearrange("b (p s) o -> p b (s o)", s=PACK))
-        xm0_raw = load_x(xm[0])
-        xT1_raw = load_x(xT[1])
-        xm1_raw = load_x(xm[1])
-
-        wg = [staged(), staged()]
-        for u in range(2):
-            cast_pairs("w", u, 0, w_raw[u, 0], HALF)
-            cast_pairs("w", u, 1, w_raw[u, 1], 384)
-            for b in range(B):
-                gather("w", u, b, wg[b])
-        xT0 = cast_xT(xT0_raw)
-        wq = [quantize("w%d" % b, wg[b], E4M3) for b in range(B)]
-        xq0 = quantize("xT0", xT0, E4M3)
-        cast_pairs("v", 0, 0, v_raw[0, 0], HALF)
-        cast_pairs("v", 0, 1, v_raw[0, 1], HALF)
-        cast_pairs("v", 1, 0, v_raw[1, 0], HALF)
-        exps0, total0 = exponentials(0, xq0, wq[0])
-        vg = [staged(), staged()]
-        for b in range(B):
-            gather("v", 0, b, vg[b])
-        cast_pairs("v", 1, 1, v_raw[1, 1], 0)
-        gather("v", 1, 0, vg[0])
+        r_v00 = load_table(vT, 0, 0)
+        r_xm1 = load_x(xm[1])
+        r_xm0 = load_x(xm[0])
+        cast_pairs("v", 1, 1, r_v11, 1024)
+        b_xT0 = cast_x(r_xT0, 0, True, 96, False, 1)
+        cast_pairs("v", 1, 0, r_v10, 1024)
+        cast_pairs("w", 0, 0, r_w00, 256)
+        cast_pairs("w", 1, 0, r_w10, 1024)
+        b_xT1 = cast_x(r_xT1, 1, True, 0, True, 1)
+        cast_pairs("w", 0, 1, r_w01, 256)
+        cast_pairs("v", 0, 0, r_v00, 768)
+        cast_pairs("v", 0, 1, r_v01, 640)
+        g_v0 = staged(next_tag("joined", 4))
+        gather("v", 0, 0, g_v0)
+        gather("v", 1, 0, g_v0)
+        q_xT0 = quantize("xT0", b_xT0, E4M3)
+        cast_pairs("w", 1, 1, r_w11, 384)
+        h_w1 = staged("picked1")
+        gather_plain("w", 0, 1, h_w1)
+        g_w0 = staged(next_tag("joined", 4))
+        gather("w", 0, 0, g_w0)
+        q_xT1 = quantize("xT1", b_xT1, E4M3)
+        gather("w", 1, 0, g_w0)
+        q_w0 = quantize("w0", g_w0, E4M3)
+        exps0, total0 = exponentials(0, q_xT0, q_w0)
         inv0, alpha0 = row_factors(0, total0)
-        vq0 = quantize("v0", vg[0], E4M3)
-        gather("v", 1, 1, vg[1])
-        xm0 = cast_xm(xm0_raw)
-        xT1 = cast_xT(xT1_raw)
-        g0 = gradient(0, xq0, vq0, exps0, inv0, alpha0)
-        vq1 = quantize("v1", vg[1], E4M3)
-        xq1 = quantize("xT1", xT1, E4M3)
-        xmq0 = quantize("xm0", xm0, E4M3)
-        exps1, total1 = exponentials(1, xq1, wq[1])
-        gq0 = quantize("g0", g0, E5M2)
-        xm1 = cast_xm(xm1_raw)
+        q_v0 = quantize("v0", g_v0, E4M3)
+        g0 = gradient_on_vector(0, q_xT0, q_v0, exps0, inv0, alpha0)
+        gather_plain("w", 1, 1, h_w1)
+        h_v1 = staged("picked1")
+        gather_plain("v", 0, 1, h_v1)
+        g_w1 = join_pairs(h_w1, False)
+        q_w1 = quantize("w1", g_w1, E4M3)
+        exps1, total1 = exponentials(1, q_xT1, q_w1)
+        b_xm0 = cast_x(r_xm0, 0, False, 128, False, 1)
+        q_xm0 = quantize("xm0", b_xm0, E4M3)
+        gather_plain("v", 1, 1, h_v1)
+        g_v1 = join_pairs(h_v1, False)
+        q_v1 = quantize("v1", g_v1, E4M3)
+        q_g0 = quantize("g0", g0, E5M2)
         inv1, alpha1 = row_factors(1, total1)
-        g1 = gradient(1, xq1, vq1, exps1, inv1, alpha1)
-        xmq1 = quantize("xm1", xm1, E4M3)
-        scatter(0, xmq0, gq0)
-        gq1 = quantize("g1", g1, E5M2)
-        scatter(1, xmq1, gq1)
+        g1 = gradient(1, q_xT1, q_v1, exps1, inv1, alpha1)
+        scatter(0, 1, q_xm0, q_g0, None)
+        scatter(0, 0, q_xm0, q_g0, None)
+        b_xm1 = cast_x(r_xm1, 1, False, 128, True, 1)
+        scatter(0, 3, q_xm0, q_g0, "u1")
+        q_xm1 = quantize("xm1", b_xm1, E4M3)
+        q_g1 = quantize("g1", g1, E5M2)
+        scatter(0, 2, q_xm0, q_g0, None)
+        scatter(1, 0, q_xm1, q_g1, None)
+        scatter(1, 3, q_xm1, q_g1, None)
+        scatter(1, 2, q_xm1, q_g1, None)
+        scatter(1, 1, q_xm1, q_g1, None)

@@ -20,6 +20,7 @@ P = 128
 PACK = 4
 HALF = T // 2
 LIST_COLS = N // 16
+SLOT = {"gw0": 5, "gw1": 6, "gv0": 1, "gv1": 8, "hw0": 1, "hw1": 0, "hv0": 3, "hv1": 2, "bxT0": 7, "bxT1": 0, "bxm0": 4, "bxm1": 0, "pl0": 6, "pl1": 0, "qw0": 2, "qw1": 0, "qv0": 3, "qv1": 0, "qxT0": 9, "qxT1": 2, "qxm0": 7, "qxm1": 5, "qg0": 6, "qg1": 9, "Pa0": 0, "Pa1": 0, "Pv0": 1, "Pv1": 1, "Pd0": 0, "Pd1": 1}
 
 
 def tile_attend_ghv_kl_kernel(tc, xT, wT, vT, wt, xm, offs, out):
@@ -82,8 +83,8 @@ def tile_attend_ghv_kl_kernel(tc, xT, wT, vT, wt, xm, offs, out):
                 in_=window.indirect(offsets[:, b * LIST_COLS : (b + 1) * LIST_COLS]),
             )
 
-        def join_pairs(src, on_gpsimd):
-            staging = staged(next_tag("joined", 4))
+        def join_pairs(name, src, on_gpsimd):
+            staging = staged("stage%d" % SLOT["g" + name])
             dst = staging[:].rearrange("p (n u e) -> p n u e", u=2, e=2)
             view = src[:].rearrange("p (u n e) -> p n u e", u=2, e=2)
             if on_gpsimd:
@@ -95,13 +96,13 @@ def tile_attend_ghv_kl_kernel(tc, xT, wT, vT, wt, xm, offs, out):
             return staging
 
         def quantize(name, src, fmt):
-            codes = keep.tile([P, N], U32, name="codes_" + name, align_bytes=64)
-            scales = keep.tile([P, N], U8, name="scales_" + name, align_bytes=64)
+            codes = keep.tile([P, N], U32, name="codes", tag="codes%d" % SLOT["q" + name], align_bytes=64)
+            scales = keep.tile([P, N], U8, name="scales", tag="scales%d" % SLOT["q" + name], align_bytes=64)
             nc.vector.quantize_mx(out=codes[:].bitcast(fmt), scales=scales[:], in_=src[:])
             return codes, scales, fmt
 
-        def product(lhs, j, rhs):
-            bank = psum.tile([P, N], F32, name="bank", tag=next_tag("bank%d" % j, 2))
+        def product(lhs, j, rhs, role):
+            bank = psum.tile([P, N], F32, name="bank", tag="bank%d_%d" % (SLOT[role], j))
             cols = slice(j * P, (j + 1) * P)
             nc.tensor.matmul_mx(
                 out=bank[:],
@@ -115,7 +116,7 @@ def tile_attend_ghv_kl_kernel(tc, xT, wT, vT, wt, xm, offs, out):
             return bank
 
         def cast_x(view, b, turned, aside, on_gpsimd, parts):
-            staging = staged("x%d" % b)
+            staging = staged("stage%d" % SLOT[("bxT%d" if turned else "bxm%d") % b])
             if turned:
                 dst = staging[:].rearrange("p (s m t) -> p m s t", s=PACK, t=PACK)
                 src = view.rearrange("p t (m s) -> p m s t", s=PACK)
@@ -137,7 +138,7 @@ def tile_attend_ghv_kl_kernel(tc, xT, wT, vT, wt, xm, offs, out):
             total = keep.tile([P, PACK], F32, name="total%d" % b)
             exps = keep.tile([P, PACK, N], F32, name="exps%d" % b, tag="exps%d" % b)
             for s in range(PACK):
-                a = product(xq, s, wq)
+                a = product(xq, s, wq, "Pa%d" % b)
                 nc.vector.tensor_reduce(out=neg_max[:, s : s + 1], in_=a[:], axis=AX.X, op=ALU.max, negate=True)
                 nc.scalar.activation(
                     out=exps[:, s, :], in_=a[:], func=ACT.Exp, bias=neg_max[:, s : s + 1], accum_out=total[:, s : s + 1]
@@ -157,7 +158,7 @@ def tile_attend_ghv_kl_kernel(tc, xT, wT, vT, wt, xm, offs, out):
             u = keep.tile([P, PACK, N], F32, name="u%d" % b, tag="u%d" % b)
             for s in range(PACK):
                 col = slice(s, s + 1)
-                av = product(xq, s, vq)
+                av = product(xq, s, vq, "Pv%d" % b)
                 nc.vector.scalar_tensor_tensor(
                     out=u[:, s, :], in0=av[:], scalar=alpha[:, col], in1=exps[:, s, :],
                     op0=ALU.mult, op1=ALU.mult, accum_out=usum[:, col],
@@ -178,7 +179,7 @@ def tile_attend_ghv_kl_kernel(tc, xT, wT, vT, wt, xm, offs, out):
             neg_beta = keep.tile([P, PACK], F32, name="neg_beta%d" % b)
             u = keep.tile([P, PACK, N], F32, name="u%d" % b, tag="u%d" % b)
             for s in range(PACK):
-                av = product(xq, s, vq)
+                av = product(xq, s, vq, "Pv%d" % b)
                 nc.vector.scalar_tensor_tensor(
                     out=u[:, s, :], in0=av[:], scalar=alpha[:, s : s + 1], in1=exps[:, s, :],
                     op0=ALU.mult, op1=ALU.mult, accum_out=usum[:, s : s + 1],
@@ -189,7 +190,7 @@ def tile_attend_ghv_kl_kernel(tc, xT, wT, vT, wt, xm, offs, out):
                         out=neg_beta[:, two], in0=usum[:, two], scalar=-1.0, in1=inv[:, two],
                         op0=ALU.mult, op1=ALU.mult,
                     )
-            planes = staged("planes")
+            planes = staged("stage%d" % SLOT["pl%d" % b])
             for s in range(PACK):
                 nc.vector.scalar_tensor_tensor(
                     out=planes[:, s * N : (s + 1) * N], in0=exps[:, s, :], scalar=neg_beta[:, s : s + 1],
@@ -203,7 +204,7 @@ def tile_attend_ghv_kl_kernel(tc, xT, wT, vT, wt, xm, offs, out):
             return g
 
         def scatter(b, j, xmq, gq, tag):
-            bank = product(xmq, j, gq)
+            bank = product(xmq, j, gq, "Pd%d" % b)
             if tag:
                 dw = keep.tile([P, N], F32, name="dw_late", tag=tag)
             else:
@@ -221,64 +222,63 @@ def tile_attend_ghv_kl_kernel(tc, xT, wT, vT, wt, xm, offs, out):
         r_w00 = load_table(wT, 0, 0)
         nc.sync.dma_start(offsets[:], offs)
         r_w01 = load_table(wT, 0, 1)
-        r_w10 = load_table(wT, 1, 0)
         r_w11 = load_table(wT, 1, 1)
-        r_xT0 = load_x(xT[0])
+        r_w10 = load_table(wT, 1, 0)
         r_xT1 = load_x(xT[1])
-        r_v10 = load_table(vT, 1, 0)
-        r_v11 = load_table(vT, 1, 1)
+        r_xT0 = load_x(xT[0])
+        r_v00 = load_table(vT, 0, 0)
         r_v01 = load_table(vT, 0, 1)
         nc.sync.dma_start(out=weights[:], in_=wt.rearrange("b (p s) o -> p b (s o)", s=PACK))
-        r_v00 = load_table(vT, 0, 0)
-        r_xm1 = load_x(xm[1])
+        r_v11 = load_table(vT, 1, 1)
+        r_v10 = load_table(vT, 1, 0)
         r_xm0 = load_x(xm[0])
-        cast_pairs("v", 1, 1, r_v11, 1024)
-        b_xT0 = cast_x(r_xT0, 0, True, 96, False, 1)
-        cast_pairs("v", 1, 0, r_v10, 1024)
-        cast_pairs("w", 0, 0, r_w00, 256)
-        cast_pairs("w", 1, 0, r_w10, 1024)
-        b_xT1 = cast_x(r_xT1, 1, True, 0, True, 1)
-        cast_pairs("w", 0, 1, r_w01, 256)
-        cast_pairs("v", 0, 0, r_v00, 768)
-        cast_pairs("v", 0, 1, r_v01, 640)
-        g_v0 = staged(next_tag("joined", 4))
-        gather("v", 0, 0, g_v0)
-        gather("v", 1, 0, g_v0)
+        r_xm1 = load_x(xm[1])
+        cast_pairs("w", 1, 0, r_w10, 512)
+        b_xT0 = cast_x(r_xT0, 0, True, 128, False, 4)
         q_xT0 = quantize("xT0", b_xT0, E4M3)
-        cast_pairs("w", 1, 1, r_w11, 384)
-        h_w1 = staged("picked1")
-        gather_plain("w", 0, 1, h_w1)
-        g_w0 = staged(next_tag("joined", 4))
+        cast_pairs("w", 0, 0, r_w00, 640)
+        cast_pairs("w", 0, 1, r_w01, 512)
+        cast_pairs("w", 1, 1, r_w11, 1024)
+        g_w0 = staged("stage%d" % SLOT["gw0"])
         gather("w", 0, 0, g_w0)
-        q_xT1 = quantize("xT1", b_xT1, E4M3)
+        b_xT1 = cast_x(r_xT1, 1, True, 64, False, 4)
+        cast_pairs("v", 0, 1, r_v01, 1024)
+        cast_pairs("v", 0, 0, r_v00, 0)
+        cast_pairs("v", 1, 0, r_v10, 1024)
+        h_v1 = staged("stage%d" % SLOT["hv1"])
+        gather_plain("v", 0, 1, h_v1)
+        cast_pairs("v", 1, 1, r_v11, 1024)
         gather("w", 1, 0, g_w0)
+        g_v0 = staged("stage%d" % SLOT["gv0"])
+        gather("v", 1, 0, g_v0)
         q_w0 = quantize("w0", g_w0, E4M3)
         exps0, total0 = exponentials(0, q_xT0, q_w0)
         inv0, alpha0 = row_factors(0, total0)
+        g_w1 = staged("stage%d" % SLOT["gw1"])
+        gather("w", 1, 1, g_w1)
+        q_xT1 = quantize("xT1", b_xT1, E4M3)
+        gather("v", 0, 0, g_v0)
         q_v0 = quantize("v0", g_v0, E4M3)
         g0 = gradient_on_vector(0, q_xT0, q_v0, exps0, inv0, alpha0)
-        gather_plain("w", 1, 1, h_w1)
-        h_v1 = staged("picked1")
-        gather_plain("v", 0, 1, h_v1)
-        g_w1 = join_pairs(h_w1, False)
-        q_w1 = quantize("w1", g_w1, E4M3)
-        exps1, total1 = exponentials(1, q_xT1, q_w1)
-        b_xm0 = cast_x(r_xm0, 0, False, 128, False, 1)
-        q_xm0 = quantize("xm0", b_xm0, E4M3)
         gather_plain("v", 1, 1, h_v1)
-        g_v1 = join_pairs(h_v1, False)
-        q_v1 = quantize("v1", g_v1, E4M3)
+        gather("w", 0, 1, g_w1)
+        b_xm0 = cast_x(r_xm0, 0, False, 128, False, 4)
         q_g0 = quantize("g0", g0, E5M2)
+        q_w1 = quantize("w1", g_w1, E4M3)
+        g_v1 = join_pairs("v1", h_v1, True)
+        q_v1 = quantize("v1", g_v1, E4M3)
+        exps1, total1 = exponentials(1, q_xT1, q_w1)
         inv1, alpha1 = row_factors(1, total1)
+        q_xm0 = quantize("xm0", b_xm0, E4M3)
         g1 = gradient(1, q_xT1, q_v1, exps1, inv1, alpha1)
-        scatter(0, 1, q_xm0, q_g0, None)
         scatter(0, 0, q_xm0, q_g0, None)
-        b_xm1 = cast_x(r_xm1, 1, False, 128, True, 1)
-        scatter(0, 3, q_xm0, q_g0, "u1")
-        q_xm1 = quantize("xm1", b_xm1, E4M3)
         q_g1 = quantize("g1", g1, E5M2)
+        b_xm1 = cast_x(r_xm1, 1, False, 128, False, 4)
+        q_xm1 = quantize("xm1", b_xm1, E4M3)
+        scatter(0, 1, q_xm0, q_g0, None)
         scatter(0, 2, q_xm0, q_g0, None)
+        scatter(0, 3, q_xm0, q_g0, "u1")
         scatter(1, 0, q_xm1, q_g1, None)
-        scatter(1, 3, q_xm1, q_g1, None)
-        scatter(1, 2, q_xm1, q_g1, None)
         scatter(1, 1, q_xm1, q_g1, None)
+        scatter(1, 2, q_xm1, q_g1, None)
+        scatter(1, 3, q_xm1, q_g1, None)

@@ -20,7 +20,7 @@ P = 128
 PACK = 4
 HALF = T // 2
 LIST_COLS = N // 16
-SLOT = {"gw0": 5, "gw1": 6, "gv0": 1, "gv1": 8, "hw0": 1, "hw1": 0, "hv0": 3, "hv1": 2, "bxT0": 7, "bxT1": 0, "bxm0": 4, "bxm1": 0, "pl0": 6, "pl1": 0, "qw0": 2, "qw1": 0, "qv0": 3, "qv1": 0, "qxT0": 9, "qxT1": 2, "qxm0": 7, "qxm1": 5, "qg0": 6, "qg1": 9, "Pa0": 0, "Pa1": 0, "Pv0": 1, "Pv1": 1, "Pd0": 0, "Pd1": 1}
+SLOT = {"gw0": 7, "gw1": 0, "gv0": 6, "gv1": 3, "hw0": 3, "hw1": 8, "hv0": 7, "hv1": 0, "bxT0": 3, "bxT1": 4, "bxm0": 4, "bxm1": 2, "pl0": 0, "pl1": 6, "qw0": 3, "qw1": 7, "qv0": 0, "qv1": 4, "qxT0": 5, "qxT1": 1, "qxm0": 0, "qxm1": 3, "qg0": 9, "qg1": 1, "Pa0": 0, "Pa1": 1, "Pv0": 0, "Pv1": 1, "Pd0": 1, "Pd1": 0}
 
 
 def tile_attend_ghv_kl_kernel(tc, xT, wT, vT, wt, xm, offs, out):
@@ -51,6 +51,26 @@ def tile_attend_ghv_kl_kernel(tc, xT, wT, vT, wt, xm, offs, out):
             rows = table.rearrange("(p t) n -> p t n", t=PACK)
             nc.sync.dma_start(out=view, in_=rows[:, 2 * u : 2 * u + 2, h * HALF : (h + 1) * HALF])
             return view
+
+        def load_table_halves(table, u, h):
+            chunk = keep.tile([P, PACK * R], F32, name="raw", tag=next_tag("raw", 8))
+            view = chunk[:].rearrange("p (q e n) -> p q e n", q=2, e=2)
+            rows = table.rearrange("(p t) n -> p t n", t=PACK)
+            for q in range(2):
+                first = h * HALF + q * HALF // 2
+                nc.sync.dma_start(out=view[:, q], in_=rows[:, 2 * u : 2 * u + 2, first : first + HALF // 2])
+            return view
+
+        def cast_pairs_halves(name, u, h, view, on_scalar):
+            for q in range(2):
+                first = h * HALF + q * HALF // 2
+                dst = pairs[name, u][:].rearrange("p (n e) -> p n e", e=2)[:, first : first + HALF // 2, :]
+                src = view[:, q].rearrange("p e n -> p n e")
+                k = on_scalar[q]
+                if k > 0:
+                    nc.scalar.activation(out=dst[:, :k, :], in_=src[:, :k, :], func=ACT.Copy)
+                if k < HALF // 2:
+                    nc.vector.tensor_copy(out=dst[:, k:, :], in_=src[:, k:, :])
 
         def load_x(x):
             chunk = keep.tile([P, PACK * R], F32, name="raw", tag=next_tag("raw", 8))
@@ -222,61 +242,64 @@ def tile_attend_ghv_kl_kernel(tc, xT, wT, vT, wt, xm, offs, out):
         r_w00 = load_table(wT, 0, 0)
         nc.sync.dma_start(offsets[:], offs)
         r_w01 = load_table(wT, 0, 1)
-        r_w11 = load_table(wT, 1, 1)
         r_w10 = load_table(wT, 1, 0)
+        r_w11 = load_table(wT, 1, 1)
         r_xT1 = load_x(xT[1])
         r_xT0 = load_x(xT[0])
         r_v00 = load_table(vT, 0, 0)
         r_v01 = load_table(vT, 0, 1)
-        nc.sync.dma_start(out=weights[:], in_=wt.rearrange("b (p s) o -> p b (s o)", s=PACK))
-        r_v11 = load_table(vT, 1, 1)
         r_v10 = load_table(vT, 1, 0)
-        r_xm0 = load_x(xm[0])
+        r_v11 = load_table_halves(vT, 1, 1)
         r_xm1 = load_x(xm[1])
-        cast_pairs("w", 1, 0, r_w10, 512)
-        b_xT0 = cast_x(r_xT0, 0, True, 128, False, 4)
-        q_xT0 = quantize("xT0", b_xT0, E4M3)
-        cast_pairs("w", 0, 0, r_w00, 640)
-        cast_pairs("w", 0, 1, r_w01, 512)
-        cast_pairs("w", 1, 1, r_w11, 1024)
-        g_w0 = staged("stage%d" % SLOT["gw0"])
-        gather("w", 0, 0, g_w0)
-        b_xT1 = cast_x(r_xT1, 1, True, 64, False, 4)
+        nc.sync.dma_start(out=weights[:], in_=wt.rearrange("b (p s) o -> p b (s o)", s=PACK))
+        r_xm0 = load_x(xm[0])
+        cast_pairs("w", 1, 0, r_w10, 640)
         cast_pairs("v", 0, 1, r_v01, 1024)
-        cast_pairs("v", 0, 0, r_v00, 0)
-        cast_pairs("v", 1, 0, r_v10, 1024)
+        cast_pairs("w", 1, 1, r_w11, 512)
+        h_w0 = staged("stage%d" % SLOT["hw0"])
+        gather_plain("w", 1, 0, h_w0)
+        cast_pairs_halves("v", 1, 1, r_v11, (512, 512))
+        h_w1 = staged("stage%d" % SLOT["hw1"])
+        gather_plain("w", 1, 1, h_w1)
+        cast_pairs("w", 0, 0, r_w00, 1024)
+        cast_pairs("v", 0, 0, r_v00, 384)
+        cast_pairs("w", 0, 1, r_w01, 512)
+        gather_plain("w", 0, 1, h_w1)
+        cast_pairs("v", 1, 0, r_v10, 640)
+        gather_plain("w", 0, 0, h_w0)
+        g_w0 = join_pairs("w0", h_w0, False)
+        h_v0 = staged("stage%d" % SLOT["hv0"])
+        gather_plain("v", 0, 0, h_v0)
+        b_xT0 = cast_x(r_xT0, 0, True, 128, False, 1)
+        q_xT0 = quantize("xT0", b_xT0, E4M3)
+        g_w1 = join_pairs("w1", h_w1, False)
         h_v1 = staged("stage%d" % SLOT["hv1"])
         gather_plain("v", 0, 1, h_v1)
-        cast_pairs("v", 1, 1, r_v11, 1024)
-        gather("w", 1, 0, g_w0)
-        g_v0 = staged("stage%d" % SLOT["gv0"])
-        gather("v", 1, 0, g_v0)
         q_w0 = quantize("w0", g_w0, E4M3)
+        gather_plain("v", 1, 0, h_v0)
+        g_v0 = join_pairs("v0", h_v0, False)
         exps0, total0 = exponentials(0, q_xT0, q_w0)
         inv0, alpha0 = row_factors(0, total0)
-        g_w1 = staged("stage%d" % SLOT["gw1"])
-        gather("w", 1, 1, g_w1)
-        q_xT1 = quantize("xT1", b_xT1, E4M3)
-        gather("v", 0, 0, g_v0)
         q_v0 = quantize("v0", g_v0, E4M3)
-        g0 = gradient_on_vector(0, q_xT0, q_v0, exps0, inv0, alpha0)
         gather_plain("v", 1, 1, h_v1)
-        gather("w", 0, 1, g_w1)
-        b_xm0 = cast_x(r_xm0, 0, False, 128, False, 4)
-        q_g0 = quantize("g0", g0, E5M2)
+        g0 = gradient_on_vector(0, q_xT0, q_v0, exps0, inv0, alpha0)
+        g_v1 = join_pairs("v1", h_v1, False)
+        b_xT1 = cast_x(r_xT1, 1, True, 64, True, 1)
+        q_xT1 = quantize("xT1", b_xT1, E4M3)
         q_w1 = quantize("w1", g_w1, E4M3)
-        g_v1 = join_pairs("v1", h_v1, True)
-        q_v1 = quantize("v1", g_v1, E4M3)
         exps1, total1 = exponentials(1, q_xT1, q_w1)
+        q_g0 = quantize("g0", g0, E5M2)
+        b_xm0 = cast_x(r_xm0, 0, False, 128, False, 1)
+        b_xm1 = cast_x(r_xm1, 1, False, 128, True, 1)
+        q_xm1 = quantize("xm1", b_xm1, E4M3)
+        q_v1 = quantize("v1", g_v1, E4M3)
         inv1, alpha1 = row_factors(1, total1)
         q_xm0 = quantize("xm0", b_xm0, E4M3)
         g1 = gradient(1, q_xT1, q_v1, exps1, inv1, alpha1)
         scatter(0, 0, q_xm0, q_g0, None)
-        q_g1 = quantize("g1", g1, E5M2)
-        b_xm1 = cast_x(r_xm1, 1, False, 128, False, 4)
-        q_xm1 = quantize("xm1", b_xm1, E4M3)
         scatter(0, 1, q_xm0, q_g0, None)
         scatter(0, 2, q_xm0, q_g0, None)
+        q_g1 = quantize("g1", g1, E5M2)
         scatter(0, 3, q_xm0, q_g0, "u1")
         scatter(1, 0, q_xm1, q_g1, None)
         scatter(1, 1, q_xm1, q_g1, None)

@@ -20,7 +20,7 @@ P = 128
 PACK = 4
 HALF = T // 2
 LIST_COLS = N // 16
-SLOT = {"gw0": 7, "gw1": 0, "gv0": 6, "gv1": 3, "hw0": 3, "hw1": 8, "hv0": 7, "hv1": 0, "bxT0": 3, "bxT1": 4, "bxm0": 4, "bxm1": 2, "pl0": 0, "pl1": 6, "qw0": 3, "qw1": 7, "qv0": 0, "qv1": 4, "qxT0": 5, "qxT1": 1, "qxm0": 0, "qxm1": 3, "qg0": 9, "qg1": 1, "Pa0": 0, "Pa1": 1, "Pv0": 0, "Pv1": 1, "Pd0": 1, "Pd1": 0}
+SLOT = {"gw0": 7, "gw1": 5, "gv0": 6, "gv1": 8, "hw0": 2, "hw1": 3, "hv0": 5, "hv1": 3, "bxT0": 3, "bxT1": 4, "bxm0": 5, "bxm1": 4, "pl0": 1, "pl1": 1, "qw0": 8, "qw1": 4, "qv0": 1, "qv1": 4, "qxT0": 6, "qxT1": 0, "qxm0": 5, "qxm1": 3, "qg0": 7, "qg1": 4, "Pa0": 0, "Pa1": 0, "Pv0": 1, "Pv1": 1, "Pd0": 1, "Pd1": 0}
 
 
 def tile_attend_ghv_kl_kernel(tc, xT, wT, vT, wt, xm, offs, out):
@@ -242,64 +242,62 @@ def tile_attend_ghv_kl_kernel(tc, xT, wT, vT, wt, xm, offs, out):
         r_w00 = load_table(wT, 0, 0)
         nc.sync.dma_start(offsets[:], offs)
         r_w01 = load_table(wT, 0, 1)
+        r_xT1 = load_x(xT[1])
         r_w10 = load_table(wT, 1, 0)
         r_w11 = load_table(wT, 1, 1)
-        r_xT1 = load_x(xT[1])
         r_xT0 = load_x(xT[0])
-        r_v00 = load_table(vT, 0, 0)
         r_v01 = load_table(vT, 0, 1)
+        nc.sync.dma_start(out=weights[:], in_=wt.rearrange("b (p s) o -> p b (s o)", s=PACK))
+        r_v00 = load_table_halves(vT, 0, 0)
         r_v10 = load_table(vT, 1, 0)
         r_v11 = load_table_halves(vT, 1, 1)
-        r_xm1 = load_x(xm[1])
-        nc.sync.dma_start(out=weights[:], in_=wt.rearrange("b (p s) o -> p b (s o)", s=PACK))
         r_xm0 = load_x(xm[0])
-        cast_pairs("w", 1, 0, r_w10, 640)
+        r_xm1 = load_x(xm[1])
         cast_pairs("v", 0, 1, r_v01, 1024)
+        cast_pairs_halves("v", 1, 1, r_v11, (512, 512))
         cast_pairs("w", 1, 1, r_w11, 512)
+        cast_pairs("w", 1, 0, r_w10, 768)
         h_w0 = staged("stage%d" % SLOT["hw0"])
         gather_plain("w", 1, 0, h_w0)
-        cast_pairs_halves("v", 1, 1, r_v11, (512, 512))
-        h_w1 = staged("stage%d" % SLOT["hw1"])
-        gather_plain("w", 1, 1, h_w1)
-        cast_pairs("w", 0, 0, r_w00, 1024)
-        cast_pairs("v", 0, 0, r_v00, 384)
+        b_xT0 = cast_x(r_xT0, 0, True, 128, True, 1)
+        b_xT1 = cast_x(r_xT1, 1, True, 128, True, 1)
+        cast_pairs_halves("v", 0, 0, r_v00, (512, 512))
         cast_pairs("w", 0, 1, r_w01, 512)
-        gather_plain("w", 0, 1, h_w1)
-        cast_pairs("v", 1, 0, r_v10, 640)
+        g_v0 = staged("stage%d" % SLOT["gv0"])
+        gather("v", 0, 0, g_v0)
+        cast_pairs("v", 1, 0, r_v10, 512)
+        gather("v", 1, 0, g_v0)
+        q_v0 = quantize("v0", g_v0, E4M3)
+        cast_pairs("w", 0, 0, r_w00, 1024)
         gather_plain("w", 0, 0, h_w0)
-        g_w0 = join_pairs("w0", h_w0, False)
-        h_v0 = staged("stage%d" % SLOT["hv0"])
-        gather_plain("v", 0, 0, h_v0)
-        b_xT0 = cast_x(r_xT0, 0, True, 128, False, 1)
         q_xT0 = quantize("xT0", b_xT0, E4M3)
-        g_w1 = join_pairs("w1", h_w1, False)
-        h_v1 = staged("stage%d" % SLOT["hv1"])
-        gather_plain("v", 0, 1, h_v1)
+        g_w0 = join_pairs("w0", h_w0, False)
+        g_w1 = staged("stage%d" % SLOT["gw1"])
+        gather("w", 0, 1, g_w1)
         q_w0 = quantize("w0", g_w0, E4M3)
-        gather_plain("v", 1, 0, h_v0)
-        g_v0 = join_pairs("v0", h_v0, False)
         exps0, total0 = exponentials(0, q_xT0, q_w0)
         inv0, alpha0 = row_factors(0, total0)
-        q_v0 = quantize("v0", g_v0, E4M3)
-        gather_plain("v", 1, 1, h_v1)
+        h_v1 = staged("stage%d" % SLOT["hv1"])
+        gather_plain("v", 0, 1, h_v1)
         g0 = gradient_on_vector(0, q_xT0, q_v0, exps0, inv0, alpha0)
-        g_v1 = join_pairs("v1", h_v1, False)
-        b_xT1 = cast_x(r_xT1, 1, True, 64, True, 1)
-        q_xT1 = quantize("xT1", b_xT1, E4M3)
-        q_w1 = quantize("w1", g_w1, E4M3)
-        exps1, total1 = exponentials(1, q_xT1, q_w1)
-        q_g0 = quantize("g0", g0, E5M2)
         b_xm0 = cast_x(r_xm0, 0, False, 128, False, 1)
-        b_xm1 = cast_x(r_xm1, 1, False, 128, True, 1)
-        q_xm1 = quantize("xm1", b_xm1, E4M3)
-        q_v1 = quantize("v1", g_v1, E4M3)
+        gather("w", 1, 1, g_w1)
+        q_w1 = quantize("w1", g_w1, E4M3)
+        gather_plain("v", 1, 1, h_v1)
+        q_xT1 = quantize("xT1", b_xT1, E4M3)
+        q_g0 = quantize("g0", g0, E5M2)
+        exps1, total1 = exponentials(1, q_xT1, q_w1)
+        g_v1 = join_pairs("v1", h_v1, True)
         inv1, alpha1 = row_factors(1, total1)
-        q_xm0 = quantize("xm0", b_xm0, E4M3)
+        q_v1 = quantize("v1", g_v1, E4M3)
         g1 = gradient(1, q_xT1, q_v1, exps1, inv1, alpha1)
+        q_xm0 = quantize("xm0", b_xm0, E4M3)
+        b_xm1 = cast_x(r_xm1, 1, False, 128, False, 1)
+        q_xm1 = quantize("xm1", b_xm1, E4M3)
+        q_g1 = quantize("g1", g1, E5M2)
         scatter(0, 0, q_xm0, q_g0, None)
         scatter(0, 1, q_xm0, q_g0, None)
         scatter(0, 2, q_xm0, q_g0, None)
-        q_g1 = quantize("g1", g1, E5M2)
         scatter(0, 3, q_xm0, q_g0, "u1")
         scatter(1, 0, q_xm1, q_g1, None)
         scatter(1, 1, q_xm1, q_g1, None)

from contextlib import ExitStack

import concourse.mybir as mybir

B, N, T, D, R = 2, 512, 2048, 512, 512
FLOPS = 3 * 2 * B * R * N * D

F32 = mybir.dt.float32
BF16 = mybir.dt.bfloat16
U32 = mybir.dt.uint32
U16 = mybir.dt.uint16
U8 = mybir.dt.uint8
E4M3 = mybir.dt.float8_e4m3fn_x4
E5M2 = mybir.dt.float8_e5m2_x4
ACT = mybir.ActivationFunctionType
ALU = mybir.AluOpType
AX = mybir.AxisListType

P = 128
PACK = 4
HALF = T // 2
LIST_COLS = N // 16
SLOT = {"gw0": 7, "gw1": 5, "gv0": 6, "gv1": 8, "hw0": 2, "hw1": 3, "hv0": 5, "hv1": 3, "bxT0": 3, "bxT1": 4, "bxm0": 5, "bxm1": 4, "pl0": 1, "pl1": 1, "qw0": 8, "qw1": 4, "qv0": 1, "qv1": 4, "qxT0": 6, "qxT1": 0, "qxm0": 5, "qxm1": 3, "qg0": 7, "qg1": 4, "Pa0": 0, "Pa1": 0, "Pv0": 1, "Pv1": 1, "Pd0": 1, "Pd1": 0}


def tile_attend_ghv_kl_kernel(tc, xT, wT, vT, wt, xm, offs, out):
    nc = tc.nc
    with ExitStack() as ctx:
        keep = ctx.enter_context(tc.tile_pool(name="keep", bufs=1))
        psum = ctx.enter_context(tc.psum_pool(name="psum", bufs=1))
        turns = {}

        def next_tag(kind, depth):
            turn = turns.get(kind, 0)
            turns[kind] = turn + 1
            return "%s_%d" % (kind, turn % depth)

        offsets = keep.tile([P, B * LIST_COLS], U16, name="offsets")
        weights = keep.tile([P, B, PACK], F32, name="weights")
        windows = [keep.tile([P, T], F32, name="window%d" % j) for j in range(D // P)]
        pairs = {}
        for name in ("w", "v"):
            for u in range(2):
                pairs[name, u] = keep.tile(
                    [P, 2 * T], BF16, name="pairs", tag="pairs_%s%d" % (name, u), align_bytes=64
                )

        def load_table(table, u, h):
            chunk = keep.tile([P, PACK * R], F32, name="raw", tag=next_tag("raw", 8))
            view = chunk[:].rearrange("p (e n) -> p e n", e=2)
            rows = table.rearrange("(p t) n -> p t n", t=PACK)
            nc.sync.dma_start(out=view, in_=rows[:, 2 * u : 2 * u + 2, h * HALF : (h + 1) * HALF])
            return view

        def load_table_halves(table, u, h):
            chunk = keep.tile([P, PACK * R], F32, name="raw", tag=next_tag("raw", 8))
            view = chunk[:].rearrange("p (q e n) -> p q e n", q=2, e=2)
            rows = table.rearrange("(p t) n -> p t n", t=PACK)
            for q in range(2):
                first = h * HALF + q * HALF // 2
                nc.sync.dma_start(out=view[:, q], in_=rows[:, 2 * u : 2 * u + 2, first : first + HALF // 2])
            return view

        def cast_pairs_halves(name, u, h, view, on_scalar):
            for q in range(2):
                first = h * HALF + q * HALF // 2
                dst = pairs[name, u][:].rearrange("p (n e) -> p n e", e=2)[:, first : first + HALF // 2, :]
                src = view[:, q].rearrange("p e n -> p n e")
                k = on_scalar[q]
                if k > 0:
                    nc.scalar.activation(out=dst[:, :k, :], in_=src[:, :k, :], func=ACT.Copy)
                if k < HALF // 2:
                    nc.vector.tensor_copy(out=dst[:, k:, :], in_=src[:, k:, :])

        def load_x(x):
            chunk = keep.tile([P, PACK * R], F32, name="raw", tag=next_tag("raw", 8))
            view = chunk[:].rearrange("p (t c) -> p t c", t=PACK)
            nc.sync.dma_start(out=view, in_=x.rearrange("(p t) c -> p t c", t=PACK))
            return view

        def cast_pairs(name, u, h, view, on_scalar):
            dst = pairs[name, u][:].rearrange("p (n e) -> p n e", e=2)[:, h * HALF : (h + 1) * HALF, :]
            src = view.rearrange("p e n -> p n e")
            if on_scalar > 0:
                nc.scalar.activation(out=dst[:, :on_scalar, :], in_=src[:, :on_scalar, :], func=ACT.Copy)
            if on_scalar < HALF:
                nc.vector.tensor_copy(out=dst[:, on_scalar:, :], in_=src[:, on_scalar:, :])

        def staged(tag):
            return keep.tile([P, PACK * N], BF16, name="staged", tag=tag, align_bytes=64)

        def gather(name, u, b, dst):
            words = dst[:].bitcast(U32).rearrange("p (n u) -> p n u", u=2)
            window = pairs[name, u][:].bitcast(U32)
            nc.vector.tensor_copy(
                out=words[:, :, u], in_=window.indirect(offsets[:, b * LIST_COLS : (b + 1) * LIST_COLS])
            )

        def gather_plain(name, u, b, dst):
            window = pairs[name, u][:].bitcast(U32)
            nc.vector.tensor_copy(
                out=dst[:].bitcast(U32)[:, u * N : (u + 1) * N],
                in_=window.indirect(offsets[:, b * LIST_COLS : (b + 1) * LIST_COLS]),
            )

        def join_pairs(name, src, on_gpsimd):
            staging = staged("stage%d" % SLOT["g" + name])
            dst = staging[:].rearrange("p (n u e) -> p n u e", u=2, e=2)
            view = src[:].rearrange("p (u n e) -> p n u e", u=2, e=2)
            if on_gpsimd:
                for q in range(2):
                    part = slice(q * N // 2, (q + 1) * N // 2)
                    nc.gpsimd.tensor_scalar(dst[:, part], view[:, part], 1.0, 0.0, ALU.mult, ALU.add)
            else:
                nc.scalar.copy(out=dst, in_=view)
            return staging

        def quantize(name, src, fmt):
            codes = keep.tile([P, N], U32, name="codes", tag="codes%d" % SLOT["q" + name], align_bytes=64)
            scales = keep.tile([P, N], U8, name="scales", tag="scales%d" % SLOT["q" + name], align_bytes=64)
            nc.vector.quantize_mx(out=codes[:].bitcast(fmt), scales=scales[:], in_=src[:])
            return codes, scales, fmt

        def product(lhs, j, rhs, role):
            bank = psum.tile([P, N], F32, name="bank", tag="bank%d_%d" % (SLOT[role], j))
            cols = slice(j * P, (j + 1) * P)
            nc.tensor.matmul_mx(
                out=bank[:],
                lhsT=lhs[0][:, cols].bitcast(lhs[2]),
                lhsT_scale=lhs[1][:, cols],
                rhs=rhs[0][:].bitcast(rhs[2]),
                rhs_scale=rhs[1][:],
                start=True,
                stop=True,
            )
            return bank

        def cast_x(view, b, turned, aside, on_gpsimd, parts):
            staging = staged("stage%d" % SLOT[("bxT%d" if turned else "bxm%d") % b])
            if turned:
                dst = staging[:].rearrange("p (s m t) -> p m s t", s=PACK, t=PACK)
                src = view.rearrange("p t (m s) -> p m s t", s=PACK)
            else:
                dst = staging[:].rearrange("p (c i t) -> p c t i", i=4, t=PACK)
                src = view.rearrange("p t (c i) -> p c t i", i=4)
            for q in range(parts if aside else 0):
                part = slice(q * aside // parts, (q + 1) * aside // parts)
                if on_gpsimd:
                    nc.gpsimd.tensor_scalar(dst[:, part], src[:, part], 1.0, 0.0, ALU.mult, ALU.add)
                else:
                    nc.scalar.activation(out=dst[:, part], in_=src[:, part], func=ACT.Copy)
            if aside < P:
                nc.vector.tensor_copy(out=dst[:, aside:], in_=src[:, aside:])
            return staging

        def exponentials(b, xq, wq):
            neg_max = keep.tile([P, PACK], F32, name="neg_max%d" % b)
            total = keep.tile([P, PACK], F32, name="total%d" % b)
            exps = keep.tile([P, PACK, N], F32, name="exps%d" % b, tag="exps%d" % b)
            for s in range(PACK):
                a = product(xq, s, wq, "Pa%d" % b)
                nc.vector.tensor_reduce(out=neg_max[:, s : s + 1], in_=a[:], axis=AX.X, op=ALU.max, negate=True)
                nc.scalar.activation(
                    out=exps[:, s, :], in_=a[:], func=ACT.Exp, bias=neg_max[:, s : s + 1], accum_out=total[:, s : s + 1]
                )
            return exps, total

        def row_factors(b, total):
            inv = keep.tile([P, PACK], F32, name="inv%d" % b)
            nc.vector.reciprocal(out=inv[:], in_=total[:])
            alpha = keep.tile([P, PACK], F32, name="alpha%d" % b)
            nc.vector.tensor_tensor(out=alpha[:], in0=inv[:], in1=weights[:, b, :], op=ALU.mult)
            return inv, alpha

        def gradient(b, xq, vq, exps, inv, alpha):
            usum = keep.tile([P, PACK], F32, name="usum%d" % b)
            beta = keep.tile([P, PACK], F32, name="beta%d" % b)
            u = keep.tile([P, PACK, N], F32, name="u%d" % b, tag="u%d" % b)
            for s in range(PACK):
                col = slice(s, s + 1)
                av = product(xq, s, vq, "Pv%d" % b)
                nc.vector.scalar_tensor_tensor(
                    out=u[:, s, :], in0=av[:], scalar=alpha[:, col], in1=exps[:, s, :],
                    op0=ALU.mult, op1=ALU.mult, accum_out=usum[:, col],
                )
                nc.scalar.activation(out=beta[:, col], in_=usum[:, col], func=ACT.Copy, scale=inv[:, col])
                nc.scalar.activation(out=exps[:, s, :], in_=exps[:, s, :], func=ACT.Copy, scale=beta[:, col])
            g = staged("pairs_w%d" % b)
            dst = g[:].rearrange("p (c i s) -> p c s i", i=4, s=PACK)
            in0 = u[:].rearrange("p s (c i) -> p c s i", i=4)
            in1 = exps[:].rearrange("p s (c i) -> p c s i", i=4)
            for q in range(4):
                part = slice(32 * q, 32 * (q + 1))
                nc.gpsimd.tensor_tensor(out=dst[:, part], in0=in0[:, part], in1=in1[:, part], op=ALU.subtract)
            return g

        def gradient_on_vector(b, xq, vq, exps, inv, alpha):
            usum = keep.tile([P, PACK], F32, name="usum%d" % b)
            neg_beta = keep.tile([P, PACK], F32, name="neg_beta%d" % b)
            u = keep.tile([P, PACK, N], F32, name="u%d" % b, tag="u%d" % b)
            for s in range(PACK):
                av = product(xq, s, vq, "Pv%d" % b)
                nc.vector.scalar_tensor_tensor(
                    out=u[:, s, :], in0=av[:], scalar=alpha[:, s : s + 1], in1=exps[:, s, :],
                    op0=ALU.mult, op1=ALU.mult, accum_out=usum[:, s : s + 1],
                )
                if s % 2 == 1:
                    two = slice(s - 1, s + 1)
                    nc.vector.scalar_tensor_tensor(
                        out=neg_beta[:, two], in0=usum[:, two], scalar=-1.0, in1=inv[:, two],
                        op0=ALU.mult, op1=ALU.mult,
                    )
            planes = staged("stage%d" % SLOT["pl%d" % b])
            for s in range(PACK):
                nc.vector.scalar_tensor_tensor(
                    out=planes[:, s * N : (s + 1) * N], in0=exps[:, s, :], scalar=neg_beta[:, s : s + 1],
                    in1=u[:, s, :], op0=ALU.mult, op1=ALU.add,
                )
            g = staged("pairs_w%d" % b)
            nc.scalar.copy(
                out=g[:].rearrange("p (c i s) -> p c s i", i=4, s=PACK),
                in_=planes[:].rearrange("p (s c i) -> p c s i", i=4, s=PACK),
            )
            return g

        def scatter(b, j, xmq, gq, tag):
            bank = product(xmq, j, gq, "Pd%d" % b)
            if tag:
                dw = keep.tile([P, N], F32, name="dw_late", tag=tag)
            else:
                dw = keep.tile([P, N], F32, name="dw", tag=next_tag("dw", 4))
            nc.scalar.copy(out=dw[:], in_=bank[:])
            nc.vector.tensor_copy(
                out=windows[j][:].indirect(offsets[:, b * LIST_COLS : (b + 1) * LIST_COLS]), in_=dw[:]
            )
            if b == B - 1:
                nc.sync.dma_start(out=out[j * P : (j + 1) * P, :], in_=windows[j][:])

        for window in windows:
            nc.vector.memset(window[:], 0.0)

        r_w00 = load_table(wT, 0, 0)
        nc.sync.dma_start(offsets[:], offs)
        r_w01 = load_table(wT, 0, 1)
        r_xT1 = load_x(xT[1])
        r_w10 = load_table(wT, 1, 0)
        r_w11 = load_table(wT, 1, 1)
        r_xT0 = load_x(xT[0])
        r_v01 = load_table(vT, 0, 1)
        nc.sync.dma_start(out=weights[:], in_=wt.rearrange("b (p s) o -> p b (s o)", s=PACK))
        r_v00 = load_table_halves(vT, 0, 0)
        r_v10 = load_table(vT, 1, 0)
        r_v11 = load_table_halves(vT, 1, 1)
        r_xm0 = load_x(xm[0])
        r_xm1 = load_x(xm[1])
        cast_pairs("v", 0, 1, r_v01, 1024)
        cast_pairs_halves("v", 1, 1, r_v11, (512, 512))
        cast_pairs("w", 1, 1, r_w11, 512)
        cast_pairs("w", 1, 0, r_w10, 768)
        h_w0 = staged("stage%d" % SLOT["hw0"])
        gather_plain("w", 1, 0, h_w0)
        b_xT0 = cast_x(r_xT0, 0, True, 128, True, 1)
        b_xT1 = cast_x(r_xT1, 1, True, 128, True, 1)
        cast_pairs_halves("v", 0, 0, r_v00, (512, 512))
        cast_pairs("w", 0, 1, r_w01, 512)
        g_v0 = staged("stage%d" % SLOT["gv0"])
        gather("v", 0, 0, g_v0)
        cast_pairs("v", 1, 0, r_v10, 512)
        gather("v", 1, 0, g_v0)
        q_v0 = quantize("v0", g_v0, E4M3)
        cast_pairs("w", 0, 0, r_w00, 1024)
        gather_plain("w", 0, 0, h_w0)
        q_xT0 = quantize("xT0", b_xT0, E4M3)
        g_w0 = join_pairs("w0", h_w0, False)
        g_w1 = staged("stage%d" % SLOT["gw1"])
        gather("w", 0, 1, g_w1)
        q_w0 = quantize("w0", g_w0, E4M3)
        exps0, total0 = exponentials(0, q_xT0, q_w0)
        inv0, alpha0 = row_factors(0, total0)
        h_v1 = staged("stage%d" % SLOT["hv1"])
        gather_plain("v", 0, 1, h_v1)
        g0 = gradient_on_vector(0, q_xT0, q_v0, exps0, inv0, alpha0)
        b_xm0 = cast_x(r_xm0, 0, False, 128, False, 1)
        gather("w", 1, 1, g_w1)
        q_w1 = quantize("w1", g_w1, E4M3)
        gather_plain("v", 1, 1, h_v1)
        q_xT1 = quantize("xT1", b_xT1, E4M3)
        q_g0 = quantize("g0", g0, E5M2)
        exps1, total1 = exponentials(1, q_xT1, q_w1)
        g_v1 = join_pairs("v1", h_v1, True)
        inv1, alpha1 = row_factors(1, total1)
        q_v1 = quantize("v1", g_v1, E4M3)
        g1 = gradient(1, q_xT1, q_v1, exps1, inv1, alpha1)
        q_xm0 = quantize("xm0", b_xm0, E4M3)
        b_xm1 = cast_x(r_xm1, 1, False, 128, False, 1)
        q_xm1 = quantize("xm1", b_xm1, E4M3)
        q_g1 = quantize("g1", g1, E5M2)
        scatter(0, 0, q_xm0, q_g0, None)
        scatter(0, 1, q_xm0, q_g0, None)
        scatter(0, 2, q_xm0, q_g0, None)
        scatter(0, 3, q_xm0, q_g0, "u1")
        scatter(1, 0, q_xm1, q_g1, None)
        scatter(1, 1, q_xm1, q_g1, None)
        scatter(1, 2, q_xm1, q_g1, None)
        scatter(1, 3, q_xm1, q_g1, None)
